import numpy as np
CORES = [73,201,329,457,330]
N = 5
C = 512
def setup_inputs(rng):
    return {"x": rng.standard_normal((N, 128, C), dtype=np.float32)}
def setup_inputs_big(rng):
    d = setup_inputs(rng)
    for k in ("x",): d[k] = (d[k].astype(np.float32) * 1048576.0).astype(d[k].dtype)
    return d
def setup_inputs_small(rng):
    d = setup_inputs(rng)
    for k in ("x",): d[k] = (d[k].astype(np.float32) * (1 / 1048576.0)).astype(d[k].dtype)
    return d
def setup_inputs_apart(rng):
    d = setup_inputs(rng)
    f = (10.0 ** rng.permutation(np.linspace(-1.5, 1.5, N))).astype(np.float32).reshape(N, 1, 1)
    for k in ("x",): d[k] = (d[k].astype(np.float32) * f).astype(d[k].dtype)
    return d
def reference(x):
    X = x.astype(np.float64)
    y = np.stack([sum(np.maximum(X[r] - X[s], 0.0) for s in range(N)) for r in range(N)])
    return {"y": y.astype(np.float32)}

@@ -1,0 +1,166 @@
+from concourse.bass import DstId, RemoteDMATransfer
+from concourse.mybir import AluOpType
+
+N = 5
+C = 512
+K = 2
+W = C // K
+
+SCRATCH = {
+    "land": ("sbuf", [128, N * C], "float32"),
+    "tmp": ("sbuf", [128, N * C], "float32"),
+    "ybuf": ("sbuf", [128, C], "float32"),
+    "cn": ("sbuf", [128, C], "float32"),
+    "px": ("psum", [128, C], "float32"),
+    "acc": ("psum", [128, C], "float32"),
+}
+SEMAPHORES = (["ld", "sent", "vs"] + ["y%d" % k for k in range(K)] + ["st%d" % k for k in range(K)]
+              + ["p%d_%d" % (s, k) for s in range(N) for k in range(K)])
+
+_CACHE = {}
+
+
+def _bits(m):
+    return [i for i in range(m.bit_length()) if (m >> i) & 1]
+
+
+def _plan(T, topo):
+    cores = list(T.cores)
+    site = lambda c: (topo.host(c), topo.chip(c))
+    sites = sorted(set(site(c) for c in cores))
+    at = {S: [c for c in cores if site(c) == S] for S in sites}
+    world = range((max(topo.host(c) for c in cores) + 1) * topo.CORES_PER_HOST)
+    free = {}
+    for S in sites:
+        rank_dies = set(topo.die(c) for c in at[S])
+        chip = [c for c in world if site(c) == S and c not in cores]
+        far_die = [c for c in chip if topo.die(c) not in rank_dies]
+        own_die = [c for c in chip if topo.die(c) in rank_dies]
+        free[S] = far_die[0::2] + far_die[1::2] + own_die[0::2] + own_die[1::2]
+    calls, eta = {}, {}
+
+    def add(core, items, cls):
+        calls.setdefault(core, []).append(items)
+        for (s, k, d) in items:
+            eta[(d, s, k)] = cls
+
+    helper_jobs = []
+    for s, cs in enumerate(cores):
+        S = site(cs)
+        near = [R for R in sites if R != S and topo.may_write(cs, at[R][0])]
+        far = [R for R in sites if R != S and R not in near]
+        relays = [R for R in near if all(topo.may_write(at[R][0], at[F][0]) for F in far)]
+        assert len(relays) == K
+        hl = [free[R].pop(0) for R in relays]
+        add(cs, [(s, k, hl[k]) for k in range(K)], 0)
+        second = []
+        for k, R in enumerate(relays):
+            for k2 in range(K):
+                if k2 != k:
+                    second.append((s, k2, at[R][0] if len(at[R]) == 1 else hl[k]))
+        add(cs, second, 1)
+        mates = [c for c in at[S] if c != cs]
+        if mates:
+            add(cs, [(s, k, c) for c in mates for k in range(K)], 0)
+        helper_jobs.append((s, relays, hl, far))
+    for (s, relays, hl, far) in helper_jobs:
+        for k, R in enumerate(relays):
+            add(hl[k], [(s, k, c) for F in far for c in at[F]], 4)
+            add(hl[k], [(s, k, c) for c in at[R]], 2)
+            if len(at[R]) > 1:
+                add(hl[k], [(s, k2, c) for k2 in range(K) if k2 != k for c in at[R]], 3)
+    masks = {}
+    arr = {}
+    for core, cl in calls.items():
+        away = [c for c in cores if site(c) != site(core) and topo.may_write(core, c)][0]
+        off = _bits(topo.mask(core, away))
+        for ci, items in enumerate(cl):
+            for stay in (False, True):
+                grp = [it for it in items if (site(it[2]) == site(core)) == stay]
+                if not grp:
+                    continue
+                pool = [e for e in _bits(topo.mask(core, grp[0][2])) if e not in off] if stay else off
+                ne = 1
+                while ne * 2 * len(grp) <= len(pool):
+                    ne *= 2
+                for i, it in enumerate(grp):
+                    eng = pool[i::len(grp)][:ne] if len(pool) % len(grp) == 0 else pool[i * ne:(i + 1) * ne]
+                    masks[(core, ci, it)] = sum(1 << e for e in eng)
+                    arr[(it[2], it[0], it[1])] = (ne, eta[(it[2], it[0], it[1])])
+    return calls, masks, arr
+
+
+def _slot(buf, s, k):
+    return buf[:, s * C + k * W: s * C + (k + 1) * W]
+
+
+def rank_program(g, core, T, topo):
+    if "p" not in _CACHE:
+        _CACHE["p"] = _plan(T, topo)
+    calls, masks, arr = _CACHE["p"]
+    rank = T.rank_of(core)
+    if rank is None and core not in calls:
+        return
+    sem = T.sem
+
+    if rank is not None:
+        g.sync.dma_start(T.land[:, rank * C:(rank + 1) * C], T.x[:]).then_inc(sem.ld, 16)
+
+    sent = 0
+    have = set()
+    for ci, items in enumerate(calls.get(core, [])):
+        for (s, k, d) in items:
+            if (s, k) in have:
+                continue
+            have.add((s, k))
+            if s == rank:
+                g.wait_ge(sem.ld, 16)
+            else:
+                g.wait_ge(sem["p%d_%d" % (s, k)], arr[(core, s, k)][0])
+        trs = []
+        for it in items:
+            (s, k, d) = it
+            rid, pid = topo.addr(d, core)
+            m = masks[(core, ci, it)]
+            trs.append(RemoteDMATransfer(dst_ids=[DstId(rid=rid, pnc=pid)], dma_engine_mask=m,
+                                         remote_sem=sem["p%d_%d" % (s, k)], src=_slot(T.land, s, k), dst=_slot(T.land, s, k)))
+            sent += len(_bits(m))
+        g.remote_dma_fused(trs, local_sem=sem.sent)
+    if sent:
+        g.wait_ge(sem.sent, sent)
+    if rank is None:
+        return
+
+    v = g.vector
+    nv = 0
+    v.memset(T.cn[:], float(N - 1)).then_inc(sem.vs, 1)
+    nv += 1
+    v.wait_ge(sem.ld, 16)
+    v.tensor_copy(T.px[:], T.land[:, rank * C:(rank + 1) * C]).then_inc(sem.vs, 1)
+    nv += 1
+    v.wait_ge(sem.vs, nv)
+    v.tensor_tensor(T.acc[:], T.px[:], T.cn[:], AluOpType.mult).then_inc(sem.vs, 1)
+    nv += 1
+    pieces = sorted((arr[(core, s, k)][1], k, s) for s in range(N) for k in range(K) if s != rank)
+    last = {}
+    for i, (_, k, s) in enumerate(pieces):
+        last[k] = i
+    for i, (_, k, s) in enumerate(pieces):
+        cols = slice(k * W, (k + 1) * W)
+        v.wait_ge(sem["p%d_%d" % (s, k)], arr[(core, s, k)][0])
+        v.wait_ge(sem.vs, nv)
+        v.tensor_tensor(_slot(T.tmp, s, k), T.px[:, cols], _slot(T.land, s, k), AluOpType.min).then_inc(sem.vs, 1)
+        nv += 1
+        v.wait_ge(sem.vs, nv)
+        if last[k] == i:
+            v.tensor_tensor(T.ybuf[:, cols], T.acc[:, cols], _slot(T.tmp, s, k), AluOpType.subtract).then_inc(sem["y%d" % k], 1)
+        else:
+            v.tensor_tensor(T.acc[:, cols], T.acc[:, cols], _slot(T.tmp, s, k), AluOpType.subtract).then_inc(sem.vs, 1)
+            nv += 1
+
+    for k in range(K):
+        q = g.sync if k % 2 == 0 else g.scalar
+        cols = slice(k * W, (k + 1) * W)
+        q.wait_ge(sem["y%d" % k], 1)
+        q.dma_start(T.y[:, cols], T.ybuf[:, cols]).then_inc(sem["st%d" % k], 16)
+        q.wait_ge(sem["st%d" % k], 16)

@@ -14,8 +14,17 @@ SCRATCH = {
     "px": ("psum", [128, C], "float32"),
     "acc": ("psum", [128, C], "float32"),
 }
-SEMAPHORES = (["ld", "sent", "vs"] + ["y%d" % k for k in range(K)] + ["st%d" % k for k in range(K)]
-              + ["p%d_%d" % (s, k) for s in range(N) for k in range(K)])
+
+
+def _sn(s, c0, c1):
+    return "p%d_%d_%d" % (s, c0, c1)
+
+
+def _blk(k):
+    return (k * W, (k + 1) * W)
+
+
+SEMAPHORES = ["ld", "sent", "vs", "yd", "st"] + [_sn(s, *_blk(k)) for s in range(N) for k in range(K)]
 
 _CACHE = {}
 
@@ -40,11 +49,12 @@ def _plan(T, topo):
     calls, eta = {}, {}
 
     def add(core, items, cls):
-        calls.setdefault(core, []).append(items)
-        for (s, k, d) in items:
-            eta[(d, s, k)] = cls
+        if items:
+            calls.setdefault(core, []).append(items)
+        for it in items:
+            eta[it] = cls
 
-    helper_jobs = []
+    jobs = []
     for s, cs in enumerate(cores):
         S = site(cs)
         near = [R for R in sites if R != S and topo.may_write(cs, at[R][0])]
@@ -52,78 +62,74 @@ def _plan(T, topo):
         relays = [R for R in near if all(topo.may_write(at[R][0], at[F][0]) for F in far)]
         assert len(relays) == K
         hl = [free[R].pop(0) for R in relays]
-        add(cs, [(s, k, hl[k]) for k in range(K)], 0)
-        second = []
+        add(cs, [(s,) + _blk(k) + (hl[k],) for k in range(K)], 0)
+        add(cs, [(s,) + _blk(k2) + (at[R][0] if len(at[R]) == 1 else hl[k],)
+                 for k, R in enumerate(relays) for k2 in range(K) if k2 != k], 1)
+        add(cs, [(s,) + _blk(k) + (c,) for c in at[S] if c != cs for k in range(K)], 0)
+        jobs.append((s, relays, hl, far))
+    for (s, relays, hl, far) in jobs:
         for k, R in enumerate(relays):
-            for k2 in range(K):
-                if k2 != k:
-                    second.append((s, k2, at[R][0] if len(at[R]) == 1 else hl[k]))
-        add(cs, second, 1)
-        mates = [c for c in at[S] if c != cs]
-        if mates:
-            add(cs, [(s, k, c) for c in mates for k in range(K)], 0)
-        helper_jobs.append((s, relays, hl, far))
-    for (s, relays, hl, far) in helper_jobs:
-        for k, R in enumerate(relays):
-            add(hl[k], [(s, k, c) for F in far for c in at[F]], 4)
-            add(hl[k], [(s, k, c) for c in at[R]], 2)
+            add(hl[k], [(s,) + _blk(k) + (c,) for F in far for c in at[F]], 4)
+            add(hl[k], [(s,) + _blk(k) + (c,) for c in at[R]], 2)
             if len(at[R]) > 1:
-                add(hl[k], [(s, k2, c) for k2 in range(K) if k2 != k for c in at[R]], 3)
-    masks = {}
-    arr = {}
+                add(hl[k], [(s,) + _blk(k2) + (c,) for k2 in range(K) if k2 != k for c in at[R]], 3)
+    masks, inc = {}, {}
     for core, cl in calls.items():
         away = [c for c in cores if site(c) != site(core) and topo.may_write(core, c)][0]
         off = _bits(topo.mask(core, away))
         for ci, items in enumerate(cl):
             for stay in (False, True):
-                grp = [it for it in items if (site(it[2]) == site(core)) == stay]
+                grp = [it for it in items if (site(it[3]) == site(core)) == stay]
                 if not grp:
                     continue
-                pool = [e for e in _bits(topo.mask(core, grp[0][2])) if e not in off] if stay else off
-                ne = 1
-                while ne * 2 * len(grp) <= len(pool):
-                    ne *= 2
+                pool = [e for e in _bits(topo.mask(core, grp[0][3])) if e not in off] if stay else off
+                if stay and all(eta[it] == 3 for it in grp):
+                    pool = _bits(topo.mask(core, grp[0][3]))
+                assert len(pool) % len(grp) == 0
                 for i, it in enumerate(grp):
-                    eng = pool[i::len(grp)][:ne] if len(pool) % len(grp) == 0 else pool[i * ne:(i + 1) * ne]
+                    eng = pool[i::len(grp)]
                     masks[(core, ci, it)] = sum(1 << e for e in eng)
-                    arr[(it[2], it[0], it[1])] = (ne, eta[(it[2], it[0], it[1])])
-    return calls, masks, arr
+                    inc.setdefault(it[3], []).append((eta[it], it[0], it[1], it[2], len(eng)))
+    return calls, masks, inc
 
 
-def _slot(buf, s, k):
-    return buf[:, s * C + k * W: s * C + (k + 1) * W]
+def _ap(buf, s, c0, c1):
+    return buf[:, s * C + c0: s * C + c1]
 
 
 def rank_program(g, core, T, topo):
     if "p" not in _CACHE:
         _CACHE["p"] = _plan(T, topo)
-    calls, masks, arr = _CACHE["p"]
+    calls, masks, inc = _CACHE["p"]
     rank = T.rank_of(core)
     if rank is None and core not in calls:
         return
     sem = T.sem
+    mine = inc.get(core, [])
 
     if rank is not None:
-        g.sync.dma_start(T.land[:, rank * C:(rank + 1) * C], T.x[:]).then_inc(sem.ld, 16)
+        g.sync.dma_start(_ap(T.land, rank, 0, C), T.x[:]).then_inc(sem.ld, 16)
 
     sent = 0
-    have = set()
+    waited = set()
     for ci, items in enumerate(calls.get(core, [])):
-        for (s, k, d) in items:
-            if (s, k) in have:
-                continue
-            have.add((s, k))
+        for (s, c0, c1, d) in items:
             if s == rank:
-                g.wait_ge(sem.ld, 16)
-            else:
-                g.wait_ge(sem["p%d_%d" % (s, k)], arr[(core, s, k)][0])
+                if "ld" not in waited:
+                    waited.add("ld")
+                    g.wait_ge(sem.ld, 16)
+                continue
+            for (_, s2, a0, a1, ne) in mine:
+                if s2 == s and a0 < c1 and c0 < a1 and (s2, a0, a1) not in waited:
+                    waited.add((s2, a0, a1))
+                    g.wait_ge(sem[_sn(s2, a0, a1)], ne)
         trs = []
         for it in items:
-            (s, k, d) = it
+            (s, c0, c1, d) = it
             rid, pid = topo.addr(d, core)
             m = masks[(core, ci, it)]
-            trs.append(RemoteDMATransfer(dst_ids=[DstId(rid=rid, pnc=pid)], dma_engine_mask=m,
-                                         remote_sem=sem["p%d_%d" % (s, k)], src=_slot(T.land, s, k), dst=_slot(T.land, s, k)))
+            trs.append(RemoteDMATransfer(dst_ids=[DstId(rid=rid, pnc=pid)], dma_engine_mask=m, remote_sem=sem[_sn(s, c0, c1)],
+                                         src=_ap(T.land, s, c0, c1), dst=_ap(T.land, s, c0, c1)))
             sent += len(_bits(m))
         g.remote_dma_fused(trs, local_sem=sem.sent)
     if sent:
@@ -136,31 +142,28 @@ def rank_program(g, core, T, topo):
     v.memset(T.cn[:], float(N - 1)).then_inc(sem.vs, 1)
     nv += 1
     v.wait_ge(sem.ld, 16)
-    v.tensor_copy(T.px[:], T.land[:, rank * C:(rank + 1) * C]).then_inc(sem.vs, 1)
+    v.tensor_copy(T.px[:], _ap(T.land, rank, 0, C)).then_inc(sem.vs, 1)
     nv += 1
     v.wait_ge(sem.vs, nv)
     v.tensor_tensor(T.acc[:], T.px[:], T.cn[:], AluOpType.mult).then_inc(sem.vs, 1)
     nv += 1
-    pieces = sorted((arr[(core, s, k)][1], k, s) for s in range(N) for k in range(K) if s != rank)
-    last = {}
-    for i, (_, k, s) in enumerate(pieces):
-        last[k] = i
-    for i, (_, k, s) in enumerate(pieces):
-        cols = slice(k * W, (k + 1) * W)
-        v.wait_ge(sem["p%d_%d" % (s, k)], arr[(core, s, k)][0])
-        v.wait_ge(sem.vs, nv)
-        v.tensor_tensor(_slot(T.tmp, s, k), T.px[:, cols], _slot(T.land, s, k), AluOpType.min).then_inc(sem.vs, 1)
-        nv += 1
-        v.wait_ge(sem.vs, nv)
-        if last[k] == i:
-            v.tensor_tensor(T.ybuf[:, cols], T.acc[:, cols], _slot(T.tmp, s, k), AluOpType.subtract).then_inc(sem["y%d" % k], 1)
-        else:
-            v.tensor_tensor(T.acc[:, cols], T.acc[:, cols], _slot(T.tmp, s, k), AluOpType.subtract).then_inc(sem.vs, 1)
+    order = sorted((max(p[0] for p in mine if p[1] == s), s) for s in range(N) if s != rank)
+    order = [s for (_, s) in order]
+    for grp in [order[i:i + 1] for i in range(len(order) - 2)] + [order[-2:]]:
+        for s in grp:
+            for (_, s2, a0, a1, ne) in mine:
+                if s2 == s:
+                    v.wait_ge(sem[_sn(s2, a0, a1)], ne)
+            v.tensor_tensor(_ap(T.tmp, s, 0, C), T.px[:], _ap(T.land, s, 0, C), AluOpType.min).then_inc(sem.vs, 1)
             nv += 1
+        for s in grp:
+            v.wait_ge(sem.vs, nv)
+            if s == order[-1]:
+                v.tensor_tensor(T.ybuf[:], T.acc[:], _ap(T.tmp, s, 0, C), AluOpType.subtract).then_inc(sem.yd, 1)
+            else:
+                v.tensor_tensor(T.acc[:], T.acc[:], _ap(T.tmp, s, 0, C), AluOpType.subtract).then_inc(sem.vs, 1)
+                nv += 1
 
-    for k in range(K):
-        q = g.sync if k % 2 == 0 else g.scalar
-        cols = slice(k * W, (k + 1) * W)
-        q.wait_ge(sem["y%d" % k], 1)
-        q.dma_start(T.y[:, cols], T.ybuf[:, cols]).then_inc(sem["st%d" % k], 16)
-        q.wait_ge(sem["st%d" % k], 16)
+    g.sync.wait_ge(sem.yd, 1)
+    g.sync.dma_start(T.y[:], T.ybuf[:]).then_inc(sem.st, 16)
+    g.sync.wait_ge(sem.st, 16)

@@ -1,16 +1,18 @@
 from concourse.bass import DstId, RemoteDMATransfer
-from concourse.mybir import AluOpType
+from concourse.mybir import AluOpType, ActivationFunctionType
 
 N = 5
 C = 512
 K = 2
 W = C // K
+H = 2
+LEAD = 64
+MAXP = 16
 
 SCRATCH = {
     "land": ("sbuf", [128, N * C], "float32"),
     "tmp": ("sbuf", [128, N * C], "float32"),
     "ybuf": ("sbuf", [128, C], "float32"),
-    "cn": ("sbuf", [128, C], "float32"),
     "px": ("psum", [128, C], "float32"),
     "acc": ("psum", [128, C], "float32"),
 }
@@ -24,7 +26,27 @@ def _blk(k):
     return (k * W, (k + 1) * W)
 
 
-SEMAPHORES = ["ld", "sent", "vs", "yd", "st"] + [_sn(s, *_blk(k)) for s in range(N) for k in range(K)]
+def _cut(a, b, j):
+    return (a + j * (b - a) // H, a + (j + 1) * (b - a) // H)
+
+
+def _lead(k, j):
+    return _cut(W - LEAD, W, j) if k == 0 else _cut(W, W + LEAD, j)
+
+
+def _rest(k, j):
+    return _cut(0, W - LEAD, j) if k == 0 else _cut(W + LEAD, C, j)
+
+
+SEGS = [(0, W - LEAD), (W - LEAD, W), (W, W + LEAD), (W + LEAD, C)]
+LOADS = [("ld0", W - LEAD, W + LEAD), ("ld1", 0, W - LEAD), ("ld2", W + LEAD, C)]
+_RANGES = [f(k, j) for f in (_lead, _rest) for k in range(K) for j in range(H)] + [_blk(k) for k in range(K)] + [(0, C)]
+
+SEMAPHORES = (["ld0", "ld1", "ld2", "sent", "vs", "va", "yd0", "yd1", "st0", "st1"]
+              + ["d%d" % i for i in range(MAXP)] + ["r%d" % i for i in range(MAXP)]
+              + [_sn(s, a, b) for s in range(N) for (a, b) in _RANGES])
+
+E_LEAD, E_CHIP, E_DIRECT, E_REST, E_SWAP = 0, 1, 2, 3, 4
 
 _CACHE = {}
 
@@ -45,7 +67,8 @@ def _plan(T, topo):
         chip = [c for c in world if site(c) == S and c not in cores]
         far_die = [c for c in chip if topo.die(c) not in rank_dies]
         own_die = [c for c in chip if topo.die(c) in rank_dies]
-        free[S] = far_die[0::2] + far_die[1::2] + own_die[0::2] + own_die[1::2]
+        own_die.sort(key=lambda c: (-min(abs(c - r) for r in at[S]), -c))
+        free[S] = far_die[0::2] + far_die[1::2] + own_die
     calls, eta = {}, {}
 
     def add(core, items, cls):
@@ -54,25 +77,36 @@ def _plan(T, topo):
         for it in items:
             eta[it] = cls
 
-    jobs = []
+    jobs, swaps, turn = [], [], {}
     for s, cs in enumerate(cores):
         S = site(cs)
         near = [R for R in sites if R != S and topo.may_write(cs, at[R][0])]
         far = [R for R in sites if R != S and R not in near]
         relays = [R for R in near if all(topo.may_write(at[R][0], at[F][0]) for F in far)]
         assert len(relays) == K
-        hl = [free[R].pop(0) for R in relays]
-        add(cs, [(s,) + _blk(k) + (hl[k],) for k in range(K)], 0)
-        add(cs, [(s,) + _blk(k2) + (at[R][0] if len(at[R]) == 1 else hl[k],)
-                 for k, R in enumerate(relays) for k2 in range(K) if k2 != k], 1)
-        add(cs, [(s,) + _blk(k) + (c,) for c in at[S] if c != cs for k in range(K)], 0)
+        hl = [[free[R].pop(0) for j in range(H)] for R in relays]
+        add(cs, [(s,) + _lead(k, j) + (hl[k][j],) for j in range(H) for k in range(K)], E_LEAD)
+        add(cs, [(s,) + _rest(k, j) + (hl[k][j],) for j in range(H) for k in range(K)], E_REST)
+        second = []
+        for k, R in enumerate(relays):
+            n = turn.get(R, 0)
+            turn[R] = n + 1
+            first = at[R][n % len(at[R])]
+            for k2 in range(K):
+                if k2 != k:
+                    second.append((s,) + _blk(k2) + (first,))
+                    swaps.append((first, [(s,) + _blk(k2) + (c,) for c in at[R] if c != first]))
+        add(cs, second, E_DIRECT)
+        add(cs, [(s, 0, C, c) for c in at[S] if c != cs], E_CHIP)
         jobs.append((s, relays, hl, far))
+    for (first, items) in swaps:
+        add(first, items, E_SWAP)
     for (s, relays, hl, far) in jobs:
         for k, R in enumerate(relays):
-            add(hl[k], [(s,) + _blk(k) + (c,) for F in far for c in at[F]], 4)
-            add(hl[k], [(s,) + _blk(k) + (c,) for c in at[R]], 2)
-            if len(at[R]) > 1:
-                add(hl[k], [(s,) + _blk(k2) + (c,) for k2 in range(K) if k2 != k for c in at[R]], 3)
+            for j in range(H):
+                for (cut, cls) in ((_lead, E_LEAD), (_rest, E_REST)):
+                    add(hl[k][j], [(s,) + cut(k, j) + (c,) for F in far for c in at[F]]
+                        + [(s,) + cut(k, j) + (c,) for c in at[R]], cls)
     masks, inc = {}, {}
     for core, cl in calls.items():
         away = [c for c in cores if site(c) != site(core) and topo.may_write(core, c)][0]
@@ -83,8 +117,10 @@ def _plan(T, topo):
                 if not grp:
                     continue
                 pool = [e for e in _bits(topo.mask(core, grp[0][3])) if e not in off] if stay else off
-                if stay and all(eta[it] == 3 for it in grp):
+                if stay and all(eta[it] == E_SWAP for it in grp):
                     pool = _bits(topo.mask(core, grp[0][3]))
+                if core not in cores:
+                    pool = pool[0::H]
                 assert len(pool) % len(grp) == 0
                 for i, it in enumerate(grp):
                     eng = pool[i::len(grp)]
@@ -95,6 +131,45 @@ def _plan(T, topo):
 
 def _ap(buf, s, c0, c1):
     return buf[:, s * C + c0: s * C + c1]
+
+
+def _units(mine):
+    us = []
+    for p in sorted(mine, key=lambda p: (p[0], p[1], p[2])):
+        w = (_sn(p[1], p[2], p[3]), p[4])
+        if us and us[-1][0] == p[0] and us[-1][1] == p[1] and us[-1][3] == p[2] and p[2] % W != 0:
+            u = us[-1]
+            us[-1] = (u[0], u[1], u[2], p[3], u[4] + [w])
+        else:
+            us.append((p[0], p[1], p[2], p[3], [w]))
+    return us
+
+
+def _order(mine):
+    hits = lambda p, h: p[2] < (h + 1) * W and h * W < p[3]
+    key = {}
+    for h in range(K):
+        cl = [p[0] for p in mine if hits(p, h)]
+        key[h] = (max(cl), cl.count(max(cl)))
+    late = max(range(K), key=lambda h: key[h])
+    order = sorted(mine, key=lambda p: (p[0], 1 if hits(p, late) else 0, p[1], p[2]))
+    last = {}
+    for i, p in enumerate(order):
+        for sg in SEGS:
+            if p[2] <= sg[0] and sg[1] <= p[3]:
+                last[sg] = i
+    runs = []
+    for i, p in enumerate(order):
+        rl = []
+        for sg in SEGS:
+            if p[2] <= sg[0] and sg[1] <= p[3]:
+                st = sg[0] // W if last[sg] == i else -1
+                if rl and rl[-1][2] == st and rl[-1][1] == sg[0]:
+                    rl[-1] = (rl[-1][0], sg[1], st)
+                else:
+                    rl.append((sg[0], sg[1], st))
+        runs.append(rl)
+    return order, late, runs
 
 
 def rank_program(g, core, T, topo):
@@ -108,16 +183,18 @@ def rank_program(g, core, T, topo):
     mine = inc.get(core, [])
 
     if rank is not None:
-        g.sync.dma_start(_ap(T.land, rank, 0, C), T.x[:]).then_inc(sem.ld, 16)
+        for (nm, a0, a1) in LOADS:
+            g.sync.dma_start(_ap(T.land, rank, a0, a1), T.x[:, a0:a1]).then_inc(sem[nm], 16)
 
     sent = 0
     waited = set()
     for ci, items in enumerate(calls.get(core, [])):
         for (s, c0, c1, d) in items:
             if s == rank:
-                if "ld" not in waited:
-                    waited.add("ld")
-                    g.wait_ge(sem.ld, 16)
+                for (nm, a0, a1) in LOADS:
+                    if a0 < c1 and c0 < a1 and nm not in waited:
+                        waited.add(nm)
+                        g.wait_ge(sem[nm], 16)
                 continue
             for (_, s2, a0, a1, ne) in mine:
                 if s2 == s and a0 < c1 and c0 < a1 and (s2, a0, a1) not in waited:
@@ -137,33 +214,55 @@ def rank_program(g, core, T, topo):
     if rank is None:
         return
 
-    v = g.vector
-    nv = 0
-    v.memset(T.cn[:], float(N - 1)).then_inc(sem.vs, 1)
-    nv += 1
-    v.wait_ge(sem.ld, 16)
-    v.tensor_copy(T.px[:], _ap(T.land, rank, 0, C)).then_inc(sem.vs, 1)
-    nv += 1
-    v.wait_ge(sem.vs, nv)
-    v.tensor_tensor(T.acc[:], T.px[:], T.cn[:], AluOpType.mult).then_inc(sem.vs, 1)
-    nv += 1
-    order = sorted((max(p[0] for p in mine if p[1] == s), s) for s in range(N) if s != rank)
-    order = [s for (_, s) in order]
-    for grp in [order[i:i + 1] for i in range(len(order) - 2)] + [order[-2:]]:
-        for s in grp:
-            for (_, s2, a0, a1, ne) in mine:
-                if s2 == s:
-                    v.wait_ge(sem[_sn(s2, a0, a1)], ne)
-            v.tensor_tensor(_ap(T.tmp, s, 0, C), T.px[:], _ap(T.land, s, 0, C), AluOpType.min).then_inc(sem.vs, 1)
-            nv += 1
-        for s in grp:
-            v.wait_ge(sem.vs, nv)
-            if s == order[-1]:
-                v.tensor_tensor(T.ybuf[:], T.acc[:], _ap(T.tmp, s, 0, C), AluOpType.subtract).then_inc(sem.yd, 1)
-            else:
-                v.tensor_tensor(T.acc[:], T.acc[:], _ap(T.tmp, s, 0, C), AluOpType.subtract).then_inc(sem.vs, 1)
-                nv += 1
+    order, late, runs = _order(_units(mine))
+    n = len(order)
+    assert n <= MAXP
 
-    g.sync.wait_ge(sem.yd, 1)
-    g.sync.dma_start(T.y[:], T.ybuf[:]).then_inc(sem.st, 16)
-    g.sync.wait_ge(sem.st, 16)
+    for i, (_, s, c0, c1, ne) in enumerate(order):
+        g.scalar.wait_ge(sem["d%d" % i], 1)
+        g.scalar.activation(_ap(T.tmp, s, c0, c1), _ap(T.tmp, s, c0, c1), ActivationFunctionType.Relu).then_inc(sem["r%d" % i], 1)
+
+    v = g.vector
+    v.memset(T.acc[:], 0.0).then_inc(sem.vs, 1)
+    for (nm, a0, a1) in LOADS:
+        v.wait_ge(sem[nm], 16)
+    v.tensor_copy(T.px[:], _ap(T.land, rank, 0, C)).then_inc(sem.vs, 1)
+    v.wait_ge(sem.vs, 2)
+    nva = [0]
+    nf = [0] * K
+
+    def emit_add(i):
+        s = order[i][1]
+        v.wait_ge(sem["r%d" % i], 1)
+        for (a0, a1, st) in runs[i]:
+            if nva[0]:
+                v.wait_ge(sem.va, nva[0])
+            if st < 0:
+                v.tensor_tensor(T.acc[:, a0:a1], T.acc[:, a0:a1], _ap(T.tmp, s, a0, a1), AluOpType.add).then_inc(sem.va, 1)
+                nva[0] += 1
+            else:
+                v.tensor_tensor(T.ybuf[:, a0:a1], T.acc[:, a0:a1], _ap(T.tmp, s, a0, a1),
+                                AluOpType.add).then_inc(sem["yd%d" % st], 1)
+                nf[st] += 1
+
+    pending = []
+    for i, (cls, s, c0, c1, ne) in enumerate(order):
+        if i and cls != order[i - 1][0]:
+            while pending:
+                emit_add(pending.pop(0))
+        for (nm, cnt) in ne:
+            v.wait_ge(sem[nm], cnt)
+        v.tensor_tensor(_ap(T.tmp, s, c0, c1), T.px[:, c0:c1], _ap(T.land, s, c0, c1), AluOpType.subtract).then_inc(sem["d%d" % i], 1)
+        pending.append(i)
+        while len(pending) > 2:
+            emit_add(pending.pop(0))
+    while pending:
+        emit_add(pending.pop(0))
+    if nva[0]:
+        v.wait_ge(sem.va, nva[0])
+
+    early = [h for h in range(K) if h != late][0]
+    for (q, h, st) in ((g.sync, early, "st0"), (g.scalar, late, "st1")):
+        q.wait_ge(sem["yd%d" % h], nf[h])
+        q.dma_start(T.y[:, h * W:(h + 1) * W], T.ybuf[:, h * W:(h + 1) * W]).then_inc(sem[st], 16)
+        q.wait_ge(sem[st], 16)

from concourse.bass import DstId, RemoteDMATransfer
from concourse.mybir import AluOpType, ActivationFunctionType

N = 5
C = 512
K = 2
W = C // K
H = 2
LEAD = 64
MAXP = 16

SCRATCH = {
    "land": ("sbuf", [128, N * C], "float32"),
    "tmp": ("sbuf", [128, N * C], "float32"),
    "ybuf": ("sbuf", [128, C], "float32"),
    "px": ("psum", [128, C], "float32"),
    "acc": ("psum", [128, C], "float32"),
}


def _sn(s, c0, c1):
    return "p%d_%d_%d" % (s, c0, c1)


def _blk(k):
    return (k * W, (k + 1) * W)


def _cut(a, b, j):
    return (a + j * (b - a) // H, a + (j + 1) * (b - a) // H)


def _lead(k, j):
    return _cut(W - LEAD, W, j) if k == 0 else _cut(W, W + LEAD, j)


def _rest(k, j):
    return _cut(0, W - LEAD, j) if k == 0 else _cut(W + LEAD, C, j)


SEGS = [(0, W - LEAD), (W - LEAD, W), (W, W + LEAD), (W + LEAD, C)]
LOADS = [("ld0", W - LEAD, W + LEAD), ("ld1", 0, W - LEAD), ("ld2", W + LEAD, C)]
_RANGES = [f(k, j) for f in (_lead, _rest) for k in range(K) for j in range(H)] + [_blk(k) for k in range(K)] + [(0, C)]

SEMAPHORES = (["ld0", "ld1", "ld2", "sent", "vs", "va", "yd0", "yd1", "st0", "st1"]
              + ["d%d" % i for i in range(MAXP)] + ["r%d" % i for i in range(MAXP)]
              + [_sn(s, a, b) for s in range(N) for (a, b) in _RANGES])

E_LEAD, E_CHIP, E_DIRECT, E_REST, E_SWAP = 0, 1, 2, 3, 4

_CACHE = {}


def _bits(m):
    return [i for i in range(m.bit_length()) if (m >> i) & 1]


def _plan(T, topo):
    cores = list(T.cores)
    site = lambda c: (topo.host(c), topo.chip(c))
    sites = sorted(set(site(c) for c in cores))
    at = {S: [c for c in cores if site(c) == S] for S in sites}
    world = range((max(topo.host(c) for c in cores) + 1) * topo.CORES_PER_HOST)
    free = {}
    for S in sites:
        rank_dies = set(topo.die(c) for c in at[S])
        chip = [c for c in world if site(c) == S and c not in cores]
        far_die = [c for c in chip if topo.die(c) not in rank_dies]
        own_die = [c for c in chip if topo.die(c) in rank_dies]
        own_die.sort(key=lambda c: (-min(abs(c - r) for r in at[S]), -c))
        free[S] = far_die[0::2] + far_die[1::2] + own_die
    calls, eta = {}, {}

    def add(core, items, cls):
        if items:
            calls.setdefault(core, []).append(items)
        for it in items:
            eta[it] = cls

    jobs, swaps, turn = [], [], {}
    for s, cs in enumerate(cores):
        S = site(cs)
        near = [R for R in sites if R != S and topo.may_write(cs, at[R][0])]
        far = [R for R in sites if R != S and R not in near]
        relays = [R for R in near if all(topo.may_write(at[R][0], at[F][0]) for F in far)]
        assert len(relays) == K
        hl = [[free[R].pop(0) for j in range(H)] for R in relays]
        add(cs, [(s,) + _lead(k, j) + (hl[k][j],) for j in range(H) for k in range(K)], E_LEAD)
        add(cs, [(s,) + _rest(k, j) + (hl[k][j],) for j in range(H) for k in range(K)], E_REST)
        second = []
        for k, R in enumerate(relays):
            n = turn.get(R, 0)
            turn[R] = n + 1
            first = at[R][n % len(at[R])]
            for k2 in range(K):
                if k2 != k:
                    second.append((s,) + _blk(k2) + (first,))
                    swaps.append((first, [(s,) + _blk(k2) + (c,) for c in at[R] if c != first]))
        add(cs, second, E_DIRECT)
        add(cs, [(s, 0, C, c) for c in at[S] if c != cs], E_CHIP)
        jobs.append((s, relays, hl, far))
    for (first, items) in swaps:
        add(first, items, E_SWAP)
    for (s, relays, hl, far) in jobs:
        for k, R in enumerate(relays):
            for j in range(H):
                for (cut, cls) in ((_lead, E_LEAD), (_rest, E_REST)):
                    add(hl[k][j], [(s,) + cut(k, j) + (c,) for F in far for c in at[F]]
                        + [(s,) + cut(k, j) + (c,) for c in at[R]], cls)
    masks, inc = {}, {}
    for core, cl in calls.items():
        away = [c for c in cores if site(c) != site(core) and topo.may_write(core, c)][0]
        off = _bits(topo.mask(core, away))
        for ci, items in enumerate(cl):
            for stay in (False, True):
                grp = [it for it in items if (site(it[3]) == site(core)) == stay]
                if not grp:
                    continue
                pool = [e for e in _bits(topo.mask(core, grp[0][3])) if e not in off] if stay else off
                if stay and all(eta[it] == E_SWAP for it in grp):
                    pool = _bits(topo.mask(core, grp[0][3]))
                if core not in cores:
                    pool = pool[0::H]
                assert len(pool) % len(grp) == 0
                for i, it in enumerate(grp):
                    eng = pool[i::len(grp)]
                    masks[(core, ci, it)] = sum(1 << e for e in eng)
                    inc.setdefault(it[3], []).append((eta[it], it[0], it[1], it[2], len(eng)))
    return calls, masks, inc


def _ap(buf, s, c0, c1):
    return buf[:, s * C + c0: s * C + c1]


def _units(mine):
    us = []
    for p in sorted(mine, key=lambda p: (p[0], p[1], p[2])):
        w = (_sn(p[1], p[2], p[3]), p[4])
        if us and us[-1][0] == p[0] and us[-1][1] == p[1] and us[-1][3] == p[2] and p[2] % W != 0:
            u = us[-1]
            us[-1] = (u[0], u[1], u[2], p[3], u[4] + [w])
        else:
            us.append((p[0], p[1], p[2], p[3], [w]))
    return us


def _order(mine):
    hits = lambda p, h: p[2] < (h + 1) * W and h * W < p[3]
    key = {}
    for h in range(K):
        cl = [p[0] for p in mine if hits(p, h)]
        key[h] = (max(cl), cl.count(max(cl)))
    late = max(range(K), key=lambda h: key[h])
    order = sorted(mine, key=lambda p: (p[0], 1 if hits(p, late) else 0, p[1], p[2]))
    last = {}
    for i, p in enumerate(order):
        for sg in SEGS:
            if p[2] <= sg[0] and sg[1] <= p[3]:
                last[sg] = i
    runs = []
    for i, p in enumerate(order):
        rl = []
        for sg in SEGS:
            if p[2] <= sg[0] and sg[1] <= p[3]:
                st = sg[0] // W if last[sg] == i else -1
                if rl and rl[-1][2] == st and rl[-1][1] == sg[0]:
                    rl[-1] = (rl[-1][0], sg[1], st)
                else:
                    rl.append((sg[0], sg[1], st))
        runs.append(rl)
    return order, late, runs


def rank_program(g, core, T, topo):
    if "p" not in _CACHE:
        _CACHE["p"] = _plan(T, topo)
    calls, masks, inc = _CACHE["p"]
    rank = T.rank_of(core)
    if rank is None and core not in calls:
        return
    sem = T.sem
    mine = inc.get(core, [])

    if rank is not None:
        for (nm, a0, a1) in LOADS:
            g.sync.dma_start(_ap(T.land, rank, a0, a1), T.x[:, a0:a1]).then_inc(sem[nm], 16)

    sent = 0
    waited = set()
    for ci, items in enumerate(calls.get(core, [])):
        for (s, c0, c1, d) in items:
            if s == rank:
                for (nm, a0, a1) in LOADS:
                    if a0 < c1 and c0 < a1 and nm not in waited:
                        waited.add(nm)
                        g.wait_ge(sem[nm], 16)
                continue
            for (_, s2, a0, a1, ne) in mine:
                if s2 == s and a0 < c1 and c0 < a1 and (s2, a0, a1) not in waited:
                    waited.add((s2, a0, a1))
                    g.wait_ge(sem[_sn(s2, a0, a1)], ne)
        trs = []
        for it in items:
            (s, c0, c1, d) = it
            rid, pid = topo.addr(d, core)
            m = masks[(core, ci, it)]
            trs.append(RemoteDMATransfer(dst_ids=[DstId(rid=rid, pnc=pid)], dma_engine_mask=m, remote_sem=sem[_sn(s, c0, c1)],
                                         src=_ap(T.land, s, c0, c1), dst=_ap(T.land, s, c0, c1)))
            sent += len(_bits(m))
        g.remote_dma_fused(trs, local_sem=sem.sent)
    if sent:
        g.wait_ge(sem.sent, sent)
    if rank is None:
        return

    order, late, runs = _order(_units(mine))
    n = len(order)
    assert n <= MAXP

    for i, (_, s, c0, c1, ne) in enumerate(order):
        g.scalar.wait_ge(sem["d%d" % i], 1)
        g.scalar.activation(_ap(T.tmp, s, c0, c1), _ap(T.tmp, s, c0, c1), ActivationFunctionType.Relu).then_inc(sem["r%d" % i], 1)

    v = g.vector
    v.memset(T.acc[:], 0.0).then_inc(sem.vs, 1)
    for (nm, a0, a1) in LOADS:
        v.wait_ge(sem[nm], 16)
    v.tensor_copy(T.px[:], _ap(T.land, rank, 0, C)).then_inc(sem.vs, 1)
    v.wait_ge(sem.vs, 2)
    nva = [0]
    nf = [0] * K

    def emit_add(i):
        s = order[i][1]
        v.wait_ge(sem["r%d" % i], 1)
        for (a0, a1, st) in runs[i]:
            if nva[0]:
                v.wait_ge(sem.va, nva[0])
            if st < 0:
                v.tensor_tensor(T.acc[:, a0:a1], T.acc[:, a0:a1], _ap(T.tmp, s, a0, a1), AluOpType.add).then_inc(sem.va, 1)
                nva[0] += 1
            else:
                v.tensor_tensor(T.ybuf[:, a0:a1], T.acc[:, a0:a1], _ap(T.tmp, s, a0, a1),
                                AluOpType.add).then_inc(sem["yd%d" % st], 1)
                nf[st] += 1

    pending = []
    for i, (cls, s, c0, c1, ne) in enumerate(order):
        if i and cls != order[i - 1][0]:
            while pending:
                emit_add(pending.pop(0))
        for (nm, cnt) in ne:
            v.wait_ge(sem[nm], cnt)
        v.tensor_tensor(_ap(T.tmp, s, c0, c1), T.px[:, c0:c1], _ap(T.land, s, c0, c1), AluOpType.subtract).then_inc(sem["d%d" % i], 1)
        pending.append(i)
        while len(pending) > 2:
            emit_add(pending.pop(0))
    while pending:
        emit_add(pending.pop(0))
    if nva[0]:
        v.wait_ge(sem.va, nva[0])

    early = [h for h in range(K) if h != late][0]
    for (q, h, st) in ((g.sync, early, "st0"), (g.scalar, late, "st1")):
        q.wait_ge(sem["yd%d" % h], nf[h])
        q.dma_start(T.y[:, h * W:(h + 1) * W], T.ybuf[:, h * W:(h + 1) * W]).then_inc(sem[st], 16)
        q.wait_ge(sem[st], 16)
